import numpy as np, ml_dtypes
CORES = [122,123,126,250,251,254,378,379,382,506,507,510]
N = 12
KB, QP = 1, 256
TAU = 16.0
def setup_inputs(rng):
    q = rng.standard_normal((N, 128, QP), dtype=np.float32) * (0.25 + np.abs(rng.standard_normal((N, 1, QP), dtype=np.float32))); k = rng.standard_normal((N, 128, KB * 128), dtype=np.float32) * (0.25 + np.abs(rng.standard_normal((N, 1, KB * 128), dtype=np.float32)))
    kn = k / np.sqrt((k ** 2).sum(axis=1, keepdims=True))
    for r in range(N):
        j = rng.integers(N, size=QP); i = rng.integers(KB * 128, size=QP)
        q[r] += rng.uniform(0, 0.8, QP).astype(np.float32) * np.sqrt((q[r] ** 2).sum(axis=0)) * kn[j, :, i].T
    return {"q": q.astype(ml_dtypes.bfloat16), "k": k.astype(ml_dtypes.bfloat16), "v": rng.standard_normal((N, 128, KB * 128), dtype=np.float32).astype(ml_dtypes.bfloat16)}
def setup_inputs_big(rng):
    d = setup_inputs(rng)
    for k in ("q", "k", "v"): d[k] = (d[k].astype(np.float32) * 1024.0).astype(d[k].dtype)
    return d
def setup_inputs_small(rng):
    d = setup_inputs(rng)
    for k in ("q", "k", "v"): d[k] = (d[k].astype(np.float32) * (1 / 1024.0)).astype(d[k].dtype)
    return d
def setup_inputs_apart(rng):
    d = setup_inputs(rng)
    f = (10.0 ** rng.permutation(np.linspace(-1.5, 1.5, N))).astype(np.float32).reshape(N, 1, 1)
    for k in ("q", "k"): d[k] = (d[k].astype(np.float32) * f).astype(d[k].dtype)
    return d
def setup_inputs_mixed(rng):
    d = setup_inputs(rng)
    for k in ("q", "k"):
        x = d[k].astype(np.float32); n = (N, 1, x.shape[2])
        f = (10.0 ** rng.uniform(-3, 3, n)).astype(np.float32); shape = rng.integers(3, size=n)
        level = np.sign(x) * np.abs(x).mean(axis=1, keepdims=True) * rng.uniform(0.9, 1.1, x.shape).astype(np.float32)
        other = x * np.where(rng.random(x.shape) < 0.75, 0.01, 1.0).astype(np.float32)
        d[k] = (np.where(shape == 1, level, np.where(shape == 2, other, x)) * f).astype(d[k].dtype)
    return d
def reference(q, k, v):
    Q, K, V = q.astype(np.float64), k.astype(np.float64), v.astype(np.float64)
    Q = Q / np.sqrt((Q ** 2).sum(axis=1, keepdims=True)); K = K / np.sqrt((K ** 2).sum(axis=1, keepdims=True))
    y = np.zeros((N, QP, 128))
    for r in range(N):
        S = TAU * np.concatenate([K[j].T @ Q[r] for j in range(N)], axis=0)
        P = np.exp(S); P = P / P.sum(axis=0)
        y[r] = P.T @ np.concatenate([V[j][:, 128 * b:128 * b + 128] for j in range(N) for b in range(KB)], axis=0)
    return {"y": y.astype(ml_dtypes.bfloat16)}

@@ -1,0 +1,249 @@
+import math
+from concourse.bass import DstId, RemoteDMATransfer
+from concourse.mybir import AluOpType, ActivationFunctionType
+
+NR = 12
+W = 272
+CL, CK, CV, C1 = 6, 8, 136, 264
+NB = 6
+
+SCRATCH = {
+    "land": ("sbuf", [128, NR, W], "bfloat16"),
+    "qs": ("sbuf", [128, 256], "bfloat16"),
+    "qsq": ("sbuf", [128, 256], "bfloat16"),
+    "ksq": ("sbuf", [128, 128], "bfloat16"),
+    "ones": ("sbuf", [128, 128], "bfloat16"),
+    "lnb": ("sbuf", [128, 260], "float32"),
+    "sc": ("sbuf", [128, 260], "float32"),
+    "lf": ("sbuf", [128, NR], "float32"),
+    "sk": ("sbuf", [128, NR], "float32"),
+    "pp": ("sbuf", [128, NR, 256], "bfloat16"),
+    "rec": ("sbuf", [128, 4], "float32"),
+    "yo": ("sbuf", [128, 2, 128], "bfloat16"),
+    "acc0": ("psum", [128, 512], "float32"),
+    "acc1": ("psum", [128, 512], "float32"),
+}
+for _b in range(NB):
+    SCRATCH["sb%d" % _b] = ("psum", [128, 512], "float32")
+
+SEMAPHORES = ["ldk", "ldv", "ldq", "ms", "sqk", "sqq", "nk", "nq", "lnk", "lnq", "sce", "his", "los", "sent",
+              "pv0", "pv1", "r0", "r1", "y0", "y1", "st0", "st1"]
+for _j in range(NR):
+    SEMAPHORES += ["akv%d" % _j, "al%d" % _j, "s%d" % _j, "z%d" % _j, "p%d" % _j, "lf%d" % _j, "ske%d" % _j]
+
+
+def _bits(m):
+    return [e for e in range(m.bit_length()) if (m >> e) & 1]
+
+
+def _mask(es):
+    return sum(1 << e for e in es)
+
+
+def _routes(T, topo):
+    cores = list(T.cores)
+    place = lambda c: (topo.host(c), topo.chip(c))
+    chips = {}
+    for r, c in enumerate(cores):
+        chips.setdefault(place(c), []).append(r)
+    routes, views = [], []
+    for j, s in enumerate(cores):
+        home = chips[place(s)]
+        a = home.index(j)
+        sw = cab = far = None
+        for pl, rs in chips.items():
+            d = cores[rs[0]]
+            if pl == place(s):
+                continue
+            if topo.same_plane(s, d):
+                sw = rs
+            elif topo.may_write(s, d):
+                cab = rs
+            else:
+                far = rs
+        kids = {s: [cores[cab[a]], cores[sw[a]]] + [cores[r] for r in home if r != j]}
+        kids[cores[cab[a]]] = [cores[r] for r in far] + [cores[r] for r in cab if r != cab[a]]
+        kids[cores[sw[a]]] = [cores[r] for r in sw if r != sw[a]]
+        routes.append(kids)
+        views.append((home, sw, cab, far, a))
+    return routes, views
+
+
+def _split(core, dests, topo, cores):
+    place = lambda c: (topo.host(c), topo.chip(c))
+    low = []
+    for d in cores:
+        if place(d) != place(core) and topo.may_write(core, d):
+            low = _bits(topo.mask(core, d))
+    by = {}
+    for d in dests:
+        by.setdefault(place(d), []).append(d)
+    away = [pl for pl in by if pl != place(core)]
+    out = []
+    for i, pl in enumerate(away):
+        n = len(low) // len(away)
+        out.append((low[i * n:(i + 1) * n], by[pl]))
+    if place(core) in by:
+        ds = by[place(core)]
+        out.append(([e for e in _bits(topo.mask(core, ds[0])) if e not in low], ds))
+    return out
+
+
+def rank_program(g, core, T, topo):
+    me = T.rank_of(core)
+    if me is None:
+        return
+    cores = list(T.cores)
+    routes, views = _routes(T, topo)
+    sem = T.sem
+    land = T.land
+    Exp, Ln = ActivationFunctionType.Exp, ActivationFunctionType.Ln
+    LN4 = math.log(4.0)
+    pe, dve, act, sp = g.tensor, g.vector, g.scalar, g.sync
+    sb = [T["sb%d" % b] for b in range(NB)]
+    acc = [T.acc0, T.acc1]
+    place = lambda c: (topo.host(c), topo.chip(c))
+
+    nkv, nl = {}, {}
+    for j, kids in enumerate(routes):
+        for snd, ds in kids.items():
+            for es, grp in _split(snd, ds, topo, cores):
+                if core in grp:
+                    nkv[j] = len(es)
+                    nl[j] = len(es) if snd == cores[j] else 0
+
+    home, sw, cab, far, a = views[me]
+    order = [me] + [r for r in home if r != me] + [sw[a], cab[a]] + [r for r in cab if r != cab[a]] \
+        + [r for r in sw if r != sw[a]] + list(far)
+
+    sp.dma_start(land[:, me, CK:CV], T.k[:, :]).then_inc(sem.ldk, 16)
+    act.dma_start(land[:, me, CV:C1], T.v[:, :]).then_inc(sem.ldv, 16)
+    sp.dma_start(T.qs[:, :], T.q[:, :]).then_inc(sem.ldq, 16)
+
+    sent = [0]
+
+    def call(parts, j, c0, c1, rsem):
+        trs = []
+        for es, grp in parts:
+            ids = []
+            for d in grp:
+                rid, pid = topo.addr(d, core)
+                ids.append(DstId(rid=rid, pnc=pid))
+            trs.append(RemoteDMATransfer(dst_ids=ids, dma_engine_mask=_mask(es), remote_sem=rsem,
+                                         srcs=[land[:, j, c0:c1]], dsts=[land[:, j, c0:c1] for _ in grp], alu_op=0))
+            sent[0] += len(es)
+        g.remote_dma_fused(trs, local_sem=sem.sent)
+
+    mine = _split(core, routes[me][core], topo, cores)
+    g.wait_ge(sem.ldk, 16)
+    g.wait_ge(sem.ldv, 16)
+    call([p for p in mine if place(p[1][0]) != place(core)], me, CK, C1, sem["akv%d" % me])
+    call([p for p in mine if place(p[1][0]) == place(core)], me, CK, C1, sem["akv%d" % me])
+    g.wait_ge(sem.his, 1)
+    g.wait_ge(sem.los, 1)
+    call(mine, me, CL, CK, sem["al%d" % me])
+    for j in (cab[a], sw[a]):
+        g.wait_ge(sem["akv%d" % j], nkv[j])
+        g.wait_ge(sem["al%d" % j], nl[j])
+        call(_split(core, routes[j][core], topo, cores), j, CL, C1, sem["akv%d" % j])
+    g.wait_ge(sem.sent, sent[0])
+
+    dve.memset(T.ones[:, :], 1.0).then_inc(sem.ms, 1)
+    dve.memset(land[:, :, C1:W], 1.0).then_inc(sem.ms, 1)
+    dve.wait_ge(sem.ldq, 16)
+    dve.tensor_tensor(T.qsq[:, :], T.qs[:, :], T.qs[:, :], AluOpType.mult).then_inc(sem.sqq, 1)
+    dve.wait_ge(sem.lnk, 1)
+    dve.tensor_copy(land[:, me, CL:CL + 1], T.lnb[:, 256:257]).then_inc(sem.his, 1)
+    dve.wait_ge(sem.his, 1)
+    dve.tensor_tensor(land[:, me, CL + 1:CK], T.lnb[:, 256:257], land[:, me, CL:CL + 1],
+                      AluOpType.subtract).then_inc(sem.los, 1)
+    for i, j in enumerate(order):
+        t = sb[i % NB]
+        if j != me:
+            if nl[j]:
+                dve.wait_ge(sem["al%d" % j], nl[j])
+            else:
+                dve.wait_ge(sem["akv%d" % j], nkv[j])
+            dve.tensor_tensor(T.lf[:, j:j + 1], land[:, j, CL:CL + 1], land[:, j, CL + 1:CK],
+                              AluOpType.add).then_inc(sem["lf%d" % j], 1)
+        dve.wait_ge(sem["s%d" % j], 1)
+        if i == 0:
+            dve.wait_ge(sem.sce, 1)
+        dve.tensor_tensor(t[:, 0:256], t[:, 0:256], T.sc[:, 0:256], AluOpType.mult).then_inc(sem["z%d" % j], 1)
+    dve.wait_ge(sem.pv0, 1)
+    dve.reciprocal(T.rec[:, 0:1], acc[0][:, 128:129]).then_inc(sem.r0, 1)
+    dve.wait_ge(sem.pv1, 1)
+    dve.reciprocal(T.rec[:, 1:2], acc[1][:, 128:129]).then_inc(sem.r1, 1)
+    dve.wait_ge(sem.r0, 1)
+    dve.tensor_scalar(T.yo[:, 0, :], acc[0][:, 0:128], T.rec[:, 0:1], None, AluOpType.mult).then_inc(sem.y0, 1)
+
+    act.wait_ge(sem.ldk, 16)
+    act.activation(T.ksq[:, :], land[:, me, CK:CV], ActivationFunctionType.Square).then_inc(sem.sqk, 1)
+    act.wait_ge(sem.nk, 1)
+    act.activation(T.lnb[:, 256:257], sb[5][:, 0:1], Ln).then_inc(sem.lnk, 1)
+    act.wait_ge(sem.nq, 1)
+    act.activation(T.lnb[:, 0:256], sb[4][:, 0:256], Ln).then_inc(sem.lnq, 1)
+    act.wait_ge(sem.lnk, 1)
+    act.wait_ge(sem.lnq, 1)
+    act.activation(T.sc[:, 0:257], T.lnb[:, 0:257], Exp, bias=LN4, scale=-0.5).then_inc(sem.sce, 1)
+    act.wait_ge(sem.sce, 1)
+    for i, j in enumerate(order):
+        t = sb[i % NB]
+        if j != me:
+            act.wait_ge(sem["lf%d" % j], 1)
+            act.activation(T.sk[:, j:j + 1], T.lf[:, j:j + 1], Exp, bias=LN4, scale=-0.5).then_inc(sem["ske%d" % j], 1)
+            act.wait_ge(sem["ske%d" % j], 1)
+            col = T.sk[:, j:j + 1]
+        else:
+            col = T.sc[:, 256:257]
+        act.wait_ge(sem["z%d" % j], 1)
+        act.activation(T.pp[:, j, :], t[:, 0:256], Exp, scale=col).then_inc(sem["p%d" % j], 1)
+    act.wait_ge(sem.r1, 1)
+    act.activation(T.yo[:, 1, :], acc[1][:, 0:128], ActivationFunctionType.Copy, scale=T.rec[:, 1:2]).then_inc(sem.y1, 1)
+    act.wait_ge(sem.y1, 1)
+    act.dma_start(T.y[128:256, :], T.yo[:, 1, :]).then_inc(sem.st1, 16)
+    act.wait_ge(sem.st1, 16)
+
+    def score(i):
+        j = order[i]
+        if j == me:
+            pe.wait_ge(sem.ldk, 16)
+            pe.wait_ge(sem.ldq, 16)
+        else:
+            pe.wait_ge(sem["akv%d" % j], nkv[j])
+        if i == 4:
+            pe.wait_ge(sem.lnq, 1)
+        if i == 5:
+            pe.wait_ge(sem.lnk, 1)
+        pe.matmul(sb[i % NB][:, 0:256], land[:, j, CK:CV], T.qs[:, :], True, True).then_inc(sem["s%d" % j], 1)
+
+    def weigh(i):
+        j = order[i]
+        pe.wait_ge(sem["p%d" % j], 1)
+        if j == me:
+            pe.wait_ge(sem.ldv, 16)
+        for h in range(2):
+            m = pe.matmul(acc[h][:, 0:129], T.pp[:, j, 128 * h:128 * h + 128], land[:, j, CV:C1 + 1],
+                          i == 0, i == NR - 1)
+            if i == NR - 1:
+                m.then_inc(sem["pv%d" % h], 1)
+
+    pe.wait_ge(sem.ms, 2)
+    pe.wait_ge(sem.sqk, 1)
+    pe.matmul(sb[5][:, 0:1], T.ksq[:, :], T.ones[:, 0:1], True, True).then_inc(sem.nk, 1)
+    score(0)
+    pe.wait_ge(sem.sqq, 1)
+    pe.matmul(sb[4][:, 0:256], T.ones[:, :], T.qsq[:, :], True, True).then_inc(sem.nq, 1)
+    score(1)
+    score(2)
+    for i in range(3):
+        weigh(i)
+    for g0 in range(3, NR, 3):
+        for i in range(g0, g0 + 3):
+            score(i)
+        for i in range(g0, g0 + 3):
+            weigh(i)
+
+    sp.wait_ge(sem.y0, 1)
+    sp.dma_start(T.y[0:128, :], T.yo[:, 0, :]).then_inc(sem.st0, 16)
+    sp.wait_ge(sem.st0, 16)

@@ -3,9 +3,14 @@ from concourse.bass import DstId, RemoteDMATransfer
 from concourse.mybir import AluOpType, ActivationFunctionType
 
 NR = 12
+NCORES = 512
 W = 272
 CL, CK, CV, C1 = 6, 8, 136, 264
 NB = 6
+OFFDIV = 1
+SW_HELPER = False
+CAB_FIRST = False
+FAR_ONCE = True
 
 SCRATCH = {
     "land": ("sbuf", [128, NR, W], "bfloat16"),
@@ -46,6 +51,10 @@ def _routes(T, topo):
     chips = {}
     for r, c in enumerate(cores):
         chips.setdefault(place(c), []).append(r)
+    spare = {}
+    for c in range(NCORES):
+        if place(c) in chips and c not in cores:
+            spare.setdefault(place(c), []).append(c)
     routes, views = [], []
     for j, s in enumerate(cores):
         home = chips[place(s)]
@@ -61,9 +70,20 @@ def _routes(T, topo):
                 cab = rs
             else:
                 far = rs
-        kids = {s: [cores[cab[a]], cores[sw[a]]] + [cores[r] for r in home if r != j]}
-        kids[cores[cab[a]]] = [cores[r] for r in far] + [cores[r] for r in cab if r != cab[a]]
-        kids[cores[sw[a]]] = [cores[r] for r in sw if r != sw[a]]
+        if SW_HELPER:
+            same = [r for r in home if topo.die(cores[r]) == topo.die(s)]
+            hs = [c for c in spare[place(cores[sw[0]])] if topo.die(c) == topo.die(s)]
+            hub = hs[same.index(j)]
+            kids = {s: [cores[cab[a]], hub] + [cores[r] for r in home if r != j]}
+            kids[hub] = [cores[r] for r in sw]
+        else:
+            kids = {s: [cores[cab[a]], cores[sw[a]]] + [cores[r] for r in home if r != j]}
+            kids[cores[sw[a]]] = [cores[r] for r in sw if r != sw[a]]
+        if FAR_ONCE:
+            kids[cores[cab[a]]] = [cores[far[a]]] + [cores[r] for r in cab if r != cab[a]]
+            kids[cores[far[a]]] = [cores[r] for r in far if r != far[a]]
+        else:
+            kids[cores[cab[a]]] = [cores[r] for r in far] + [cores[r] for r in cab if r != cab[a]]
         routes.append(kids)
         views.append((home, sw, cab, far, a))
     return routes, views
@@ -81,8 +101,10 @@ def _split(core, dests, topo, cores):
     away = [pl for pl in by if pl != place(core)]
     out = []
     for i, pl in enumerate(away):
-        n = len(low) // len(away)
-        out.append((low[i * n:(i + 1) * n], by[pl]))
+        n = len(low) if CAB_FIRST else len(low) // len(away)
+        n = n // OFFDIV
+        k = 0 if CAB_FIRST else i
+        out.append((low[k * n:(k + 1) * n], by[pl]))
     if place(core) in by:
         ds = by[place(core)]
         out.append(([e for e in _bits(topo.mask(core, ds[0])) if e not in low], ds))
@@ -90,18 +112,13 @@ def _split(core, dests, topo, cores):
 
 
 def rank_program(g, core, T, topo):
-    me = T.rank_of(core)
-    if me is None:
-        return
     cores = list(T.cores)
     routes, views = _routes(T, topo)
+    me = T.rank_of(core)
+    if me is None and not any(core in kids for kids in routes):
+        return
     sem = T.sem
     land = T.land
-    Exp, Ln = ActivationFunctionType.Exp, ActivationFunctionType.Ln
-    LN4 = math.log(4.0)
-    pe, dve, act, sp = g.tensor, g.vector, g.scalar, g.sync
-    sb = [T["sb%d" % b] for b in range(NB)]
-    acc = [T.acc0, T.acc1]
     place = lambda c: (topo.host(c), topo.chip(c))
 
     nkv, nl = {}, {}
@@ -111,14 +128,6 @@ def rank_program(g, core, T, topo):
                 if core in grp:
                     nkv[j] = len(es)
                     nl[j] = len(es) if snd == cores[j] else 0
-
-    home, sw, cab, far, a = views[me]
-    order = [me] + [r for r in home if r != me] + [sw[a], cab[a]] + [r for r in cab if r != cab[a]] \
-        + [r for r in sw if r != sw[a]] + list(far)
-
-    sp.dma_start(land[:, me, CK:CV], T.k[:, :]).then_inc(sem.ldk, 16)
-    act.dma_start(land[:, me, CV:C1], T.v[:, :]).then_inc(sem.ldv, 16)
-    sp.dma_start(T.qs[:, :], T.q[:, :]).then_inc(sem.ldq, 16)
 
     sent = [0]
 
@@ -134,19 +143,57 @@ def rank_program(g, core, T, topo):
             sent[0] += len(es)
         g.remote_dma_fused(trs, local_sem=sem.sent)
 
+    def forwards():
+        js = [j for j, kids in enumerate(routes) if core in kids and cores[j] != core]
+        js.sort(key=lambda j: 0 if any(place(d) != place(core) for d in routes[j][core]) else (1 if nl[j] else 2))
+        for j in js:
+            g.wait_ge(sem["akv%d" % j], nkv[j])
+            if nl[j]:
+                g.wait_ge(sem["al%d" % j], nl[j])
+            call(_split(core, routes[j][core], topo, cores), j, CL, C1, sem["akv%d" % j])
+        g.wait_ge(sem.sent, sent[0])
+
+    if me is None:
+        forwards()
+        return
+
+    Exp, Ln = ActivationFunctionType.Exp, ActivationFunctionType.Ln
+    LN4 = math.log(4.0)
+    pe, dve, act, sp = g.tensor, g.vector, g.scalar, g.sync
+    sb = [T["sb%d" % b] for b in range(NB)]
+    acc = [T.acc0, T.acc1]
+
+    home, sw, cab, far, a = views[me]
+    last = [far[a]] + [r for r in far if r != far[a]]
+    if SW_HELPER:
+        order = [me] + [r for r in home if r != me] + [cab[a]] + [r for r in cab if r != cab[a]] + list(sw) + last
+    else:
+        order = [me] + [r for r in home if r != me] + [sw[a], cab[a]] + [r for r in cab if r != cab[a]] \
+            + [r for r in sw if r != sw[a]] + last
+
+    sp.dma_start(land[:, me, CK:CV], T.k[:, :]).then_inc(sem.ldk, 16)
+    act.dma_start(land[:, me, CV:C1], T.v[:, :]).then_inc(sem.ldv, 16)
+    sp.dma_start(T.qs[:, :], T.q[:, :]).then_inc(sem.ldq, 16)
+
     mine = _split(core, routes[me][core], topo, cores)
+    off = [p for p in mine if place(p[1][0]) != place(core)]
+    on = [p for p in mine if place(p[1][0]) == place(core)]
     g.wait_ge(sem.ldk, 16)
     g.wait_ge(sem.ldv, 16)
-    call([p for p in mine if place(p[1][0]) != place(core)], me, CK, C1, sem["akv%d" % me])
-    call([p for p in mine if place(p[1][0]) == place(core)], me, CK, C1, sem["akv%d" % me])
+    if CAB_FIRST:
+        for p in off:
+            call([p], me, CK, C1, sem["akv%d" % me])
+    else:
+        call(off, me, CK, C1, sem["akv%d" % me])
+    call(on, me, CK, C1, sem["akv%d" % me])
     g.wait_ge(sem.his, 1)
     g.wait_ge(sem.los, 1)
-    call(mine, me, CL, CK, sem["al%d" % me])
-    for j in (cab[a], sw[a]):
-        g.wait_ge(sem["akv%d" % j], nkv[j])
-        g.wait_ge(sem["al%d" % j], nl[j])
-        call(_split(core, routes[j][core], topo, cores), j, CL, C1, sem["akv%d" % j])
-    g.wait_ge(sem.sent, sent[0])
+    if CAB_FIRST:
+        call([off[0]] + on, me, CL, CK, sem["al%d" % me])
+        call([off[1]], me, CL, CK, sem["al%d" % me])
+    else:
+        call(mine, me, CL, CK, sem["al%d" % me])
+    forwards()
 
     dve.memset(T.ones[:, :], 1.0).then_inc(sem.ms, 1)
     dve.memset(land[:, :, C1:W], 1.0).then_inc(sem.ms, 1)
@@ -236,13 +283,13 @@ def rank_program(g, core, T, topo):
     pe.matmul(sb[4][:, 0:256], T.ones[:, :], T.qsq[:, :], True, True).then_inc(sem.nq, 1)
     score(1)
     score(2)
-    for i in range(3):
-        weigh(i)
     for g0 in range(3, NR, 3):
         for i in range(g0, g0 + 3):
             score(i)
-        for i in range(g0, g0 + 3):
+        for i in range(g0 - 3, g0):
             weigh(i)
+    for i in range(NR - 3, NR):
+        weigh(i)
 
     sp.wait_ge(sem.y0, 1)
     sp.dma_start(T.y[0:128, :], T.yo[:, 0, :]).then_inc(sem.st0, 16)

@@ -1,26 +1,24 @@
-import math
 from concourse.bass import DstId, RemoteDMATransfer
 from concourse.mybir import AluOpType, ActivationFunctionType
 
 NR = 12
-NCORES = 512
 W = 272
 CL, CK, CV, C1 = 6, 8, 136, 264
 NB = 6
-OFFDIV = 1
-SW_HELPER = False
-CAB_FIRST = False
-FAR_ONCE = True
+NRAW = 5
+PLAN = [("S", 3), ("S", 4), ("W", 0), ("W", 1), ("W", 2), ("S", 5), ("S", 6), ("W", 3), ("W", 4), ("S", 7), ("S", 8),
+        ("W", 5), ("W", 6), ("S", 9), ("W", 7), ("W", 8), ("W", 9), ("S", 10), ("S", 11), ("W", 10), ("W", 11)]
+WAVES = [[0], [1, 2], [3, 4], [5, 6, 7], [8, 9], [10, 11]]
 
 SCRATCH = {
     "land": ("sbuf", [128, NR, W], "bfloat16"),
     "qs": ("sbuf", [128, 256], "bfloat16"),
+    "qh": ("sbuf", [128, 256], "bfloat16"),
     "qsq": ("sbuf", [128, 256], "bfloat16"),
     "ksq": ("sbuf", [128, 128], "bfloat16"),
     "ones": ("sbuf", [128, 128], "bfloat16"),
     "lnb": ("sbuf", [128, 260], "float32"),
     "sc": ("sbuf", [128, 260], "float32"),
-    "lf": ("sbuf", [128, NR], "float32"),
     "sk": ("sbuf", [128, NR], "float32"),
     "pp": ("sbuf", [128, NR, 256], "bfloat16"),
     "rec": ("sbuf", [128, 4], "float32"),
@@ -32,9 +30,9 @@ for _b in range(NB):
     SCRATCH["sb%d" % _b] = ("psum", [128, 512], "float32")
 
 SEMAPHORES = ["ldk", "ldv", "ldq", "ms", "sqk", "sqq", "nk", "nq", "lnk", "lnq", "sce", "his", "los", "sent",
-              "pv0", "pv1", "r0", "r1", "y0", "y1", "st0", "st1"]
+              "pv0", "pv1", "r0", "r1", "y0", "y1", "st0", "st1", "qhs"]
 for _j in range(NR):
-    SEMAPHORES += ["akv%d" % _j, "al%d" % _j, "s%d" % _j, "z%d" % _j, "p%d" % _j, "lf%d" % _j, "ske%d" % _j]
+    SEMAPHORES += ["akv%d" % _j, "al%d" % _j, "s%d" % _j, "z%d" % _j, "p%d" % _j, "ske%d" % _j]
 
 
 def _bits(m):
@@ -51,10 +49,6 @@ def _routes(T, topo):
     chips = {}
     for r, c in enumerate(cores):
         chips.setdefault(place(c), []).append(r)
-    spare = {}
-    for c in range(NCORES):
-        if place(c) in chips and c not in cores:
-            spare.setdefault(place(c), []).append(c)
     routes, views = [], []
     for j, s in enumerate(cores):
         home = chips[place(s)]
@@ -70,23 +64,22 @@ def _routes(T, topo):
                 cab = rs
             else:
                 far = rs
-        if SW_HELPER:
-            same = [r for r in home if topo.die(cores[r]) == topo.die(s)]
-            hs = [c for c in spare[place(cores[sw[0]])] if topo.die(c) == topo.die(s)]
-            hub = hs[same.index(j)]
-            kids = {s: [cores[cab[a]], hub] + [cores[r] for r in home if r != j]}
-            kids[hub] = [cores[r] for r in sw]
-        else:
-            kids = {s: [cores[cab[a]], cores[sw[a]]] + [cores[r] for r in home if r != j]}
-            kids[cores[sw[a]]] = [cores[r] for r in sw if r != sw[a]]
-        if FAR_ONCE:
-            kids[cores[cab[a]]] = [cores[far[a]]] + [cores[r] for r in cab if r != cab[a]]
-            kids[cores[far[a]]] = [cores[r] for r in far if r != far[a]]
-        else:
-            kids[cores[cab[a]]] = [cores[r] for r in far] + [cores[r] for r in cab if r != cab[a]]
+        kids = {s: [cores[cab[a]], cores[sw[a]]] + [cores[r] for r in home if r != j]}
+        kids[cores[sw[a]]] = [cores[r] for r in sw if r != sw[a]]
+        kids[cores[cab[a]]] = [cores[far[a]]] + [cores[r] for r in cab if r != cab[a]]
+        kids[cores[far[a]]] = [cores[r] for r in far if r != far[a]]
         routes.append(kids)
         views.append((home, sw, cab, far, a))
     return routes, views
+
+
+def _pair(home, cores, topo):
+    dies = {}
+    for r in home:
+        dies.setdefault(topo.die(cores[r]), []).append(r)
+    many = [rs for rs in dies.values() if len(rs) > 1]
+    lone = [rs for rs in dies.values() if len(rs) == 1]
+    return (many[0][-1], lone[0][0]) if many and lone else (None, None)
 
 
 def _split(core, dests, topo, cores):
@@ -101,10 +94,8 @@ def _split(core, dests, topo, cores):
     away = [pl for pl in by if pl != place(core)]
     out = []
     for i, pl in enumerate(away):
-        n = len(low) if CAB_FIRST else len(low) // len(away)
-        n = n // OFFDIV
-        k = 0 if CAB_FIRST else i
-        out.append((low[k * n:(k + 1) * n], by[pl]))
+        n = len(low) // len(away)
+        out.append((low[i * n:(i + 1) * n], by[pl]))
     if place(core) in by:
         ds = by[place(core)]
         out.append(([e for e in _bits(topo.mask(core, ds[0])) if e not in low], ds))
@@ -113,13 +104,15 @@ def _split(core, dests, topo, cores):
 
 def rank_program(g, core, T, topo):
     cores = list(T.cores)
-    routes, views = _routes(T, topo)
     me = T.rank_of(core)
-    if me is None and not any(core in kids for kids in routes):
+    if me is None:
         return
+    routes, views = _routes(T, topo)
     sem = T.sem
     land = T.land
     place = lambda c: (topo.host(c), topo.chip(c))
+    home, sw, cab, far, a = views[me]
+    donor, relay = _pair(home, cores, topo)
 
     nkv, nl = {}, {}
     for j, kids in enumerate(routes):
@@ -128,6 +121,8 @@ def rank_program(g, core, T, topo):
                 if core in grp:
                     nkv[j] = len(es)
                     nl[j] = len(es) if snd == cores[j] else 0
+    if cab[a] == _pair(cab, cores, topo)[0]:
+        nkv[cab[a]] *= 2
 
     sent = [0]
 
@@ -153,23 +148,13 @@ def rank_program(g, core, T, topo):
             call(_split(core, routes[j][core], topo, cores), j, CL, C1, sem["akv%d" % j])
         g.wait_ge(sem.sent, sent[0])
 
-    if me is None:
-        forwards()
-        return
-
     Exp, Ln = ActivationFunctionType.Exp, ActivationFunctionType.Ln
-    LN4 = math.log(4.0)
     pe, dve, act, sp = g.tensor, g.vector, g.scalar, g.sync
     sb = [T["sb%d" % b] for b in range(NB)]
     acc = [T.acc0, T.acc1]
 
-    home, sw, cab, far, a = views[me]
-    last = [far[a]] + [r for r in far if r != far[a]]
-    if SW_HELPER:
-        order = [me] + [r for r in home if r != me] + [cab[a]] + [r for r in cab if r != cab[a]] + list(sw) + last
-    else:
-        order = [me] + [r for r in home if r != me] + [sw[a], cab[a]] + [r for r in cab if r != cab[a]] \
-            + [r for r in sw if r != sw[a]] + last
+    order = [me] + [r for r in home if r != me] + [sw[a], cab[a]] + [r for r in cab if r != cab[a]] \
+        + [far[a]] + [r for r in sw if r != sw[a]] + [r for r in far if r != far[a]]
 
     sp.dma_start(land[:, me, CK:CV], T.k[:, :]).then_inc(sem.ldk, 16)
     act.dma_start(land[:, me, CV:C1], T.v[:, :]).then_inc(sem.ldv, 16)
@@ -180,19 +165,18 @@ def rank_program(g, core, T, topo):
     on = [p for p in mine if place(p[1][0]) == place(core)]
     g.wait_ge(sem.ldk, 16)
     g.wait_ge(sem.ldv, 16)
-    if CAB_FIRST:
-        for p in off:
-            call([p], me, CK, C1, sem["akv%d" % me])
+    if me == donor:
+        call(off[1:] + on, me, CK, C1, sem["akv%d" % me])
+        call(off[:1], me, CK, CV, sem["akv%d" % me])
     else:
         call(off, me, CK, C1, sem["akv%d" % me])
-    call(on, me, CK, C1, sem["akv%d" % me])
+        call(on, me, CK, C1, sem["akv%d" % me])
+    if me == relay:
+        g.wait_ge(sem["akv%d" % donor], nkv[donor])
+        call([(off[0][0], [cores[views[donor][2][views[donor][4]]]])], donor, CV, C1, sem["akv%d" % donor])
     g.wait_ge(sem.his, 1)
     g.wait_ge(sem.los, 1)
-    if CAB_FIRST:
-        call([off[0]] + on, me, CL, CK, sem["al%d" % me])
-        call([off[1]], me, CL, CK, sem["al%d" % me])
-    else:
-        call(mine, me, CL, CK, sem["al%d" % me])
+    call(mine, me, CL, CK, sem["al%d" % me])
     forwards()
 
     dve.memset(T.ones[:, :], 1.0).then_inc(sem.ms, 1)
@@ -200,23 +184,17 @@ def rank_program(g, core, T, topo):
     dve.wait_ge(sem.ldq, 16)
     dve.tensor_tensor(T.qsq[:, :], T.qs[:, :], T.qs[:, :], AluOpType.mult).then_inc(sem.sqq, 1)
     dve.wait_ge(sem.lnk, 1)
-    dve.tensor_copy(land[:, me, CL:CL + 1], T.lnb[:, 256:257]).then_inc(sem.his, 1)
     dve.wait_ge(sem.his, 1)
-    dve.tensor_tensor(land[:, me, CL + 1:CK], T.lnb[:, 256:257], land[:, me, CL:CL + 1],
-                      AluOpType.subtract).then_inc(sem.los, 1)
-    for i, j in enumerate(order):
-        t = sb[i % NB]
-        if j != me:
-            if nl[j]:
-                dve.wait_ge(sem["al%d" % j], nl[j])
-            else:
-                dve.wait_ge(sem["akv%d" % j], nkv[j])
-            dve.tensor_tensor(T.lf[:, j:j + 1], land[:, j, CL:CL + 1], land[:, j, CL + 1:CK],
-                              AluOpType.add).then_inc(sem["lf%d" % j], 1)
+    dve.tensor_scalar(land[:, me, CL + 1:CK], T.lnb[:, 256:257], land[:, me, CL:CL + 1], -0.5,
+                      AluOpType.subtract, AluOpType.mult).then_inc(sem.los, 1)
+    for i in range(NRAW):
+        j, t = order[i], sb[i % NB]
         dve.wait_ge(sem["s%d" % j], 1)
         if i == 0:
             dve.wait_ge(sem.sce, 1)
         dve.tensor_tensor(t[:, 0:256], t[:, 0:256], T.sc[:, 0:256], AluOpType.mult).then_inc(sem["z%d" % j], 1)
+        if i == 2:
+            dve.tensor_tensor(T.qh[:, :], T.qs[:, :], T.sc[:, 0:256], AluOpType.mult).then_inc(sem.qhs, 1)
     dve.wait_ge(sem.pv0, 1)
     dve.reciprocal(T.rec[:, 0:1], acc[0][:, 128:129]).then_inc(sem.r0, 1)
     dve.wait_ge(sem.pv1, 1)
@@ -227,24 +205,28 @@ def rank_program(g, core, T, topo):
     act.wait_ge(sem.ldk, 16)
     act.activation(T.ksq[:, :], land[:, me, CK:CV], ActivationFunctionType.Square).then_inc(sem.sqk, 1)
     act.wait_ge(sem.nk, 1)
-    act.activation(T.lnb[:, 256:257], sb[5][:, 0:1], Ln).then_inc(sem.lnk, 1)
+    act.activation(T.lnb[:, 256:257], sb[5][:, 0:1], Ln, scale=1.0 / 16).then_inc(sem.lnk, 1)
+    act.activation(land[:, me, CL:CL + 1], sb[5][:, 0:1], Ln, scale=1.0 / 16).then_inc(sem.his, 1)
     act.wait_ge(sem.nq, 1)
-    act.activation(T.lnb[:, 0:256], sb[4][:, 0:256], Ln).then_inc(sem.lnq, 1)
+    act.activation(T.lnb[:, 0:256], sb[4][:, 0:256], Ln, scale=1.0 / 16).then_inc(sem.lnq, 1)
     act.wait_ge(sem.lnk, 1)
     act.wait_ge(sem.lnq, 1)
-    act.activation(T.sc[:, 0:257], T.lnb[:, 0:257], Exp, bias=LN4, scale=-0.5).then_inc(sem.sce, 1)
+    act.activation(T.sc[:, 0:257], T.lnb[:, 0:257], Exp, scale=-0.5).then_inc(sem.sce, 1)
     act.wait_ge(sem.sce, 1)
-    for i, j in enumerate(order):
-        t = sb[i % NB]
-        if j != me:
-            act.wait_ge(sem["lf%d" % j], 1)
-            act.activation(T.sk[:, j:j + 1], T.lf[:, j:j + 1], Exp, bias=LN4, scale=-0.5).then_inc(sem["ske%d" % j], 1)
-            act.wait_ge(sem["ske%d" % j], 1)
-            col = T.sk[:, j:j + 1]
-        else:
-            col = T.sc[:, 256:257]
-        act.wait_ge(sem["z%d" % j], 1)
-        act.activation(T.pp[:, j, :], t[:, 0:256], Exp, scale=col).then_inc(sem["p%d" % j], 1)
+    for wave in WAVES:
+        for i in wave:
+            j = order[i]
+            if j != me:
+                act.wait_ge(sem[("al%d" if nl[j] else "akv%d") % j], nl[j] or nkv[j])
+                act.activation(T.sk[:, j:j + 1], land[:, j, CL:CL + 1], Exp, bias=land[:, j, CL + 1:CK],
+                               scale=-0.5).then_inc(sem["ske%d" % j], 1)
+        for i in wave:
+            j = order[i]
+            if j != me:
+                act.wait_ge(sem["ske%d" % j], 1)
+            col = T.sk[:, j:j + 1] if j != me else T.sc[:, 256:257]
+            act.wait_ge(sem[("z%d" if i < NRAW else "s%d") % j], 1)
+            act.activation(T.pp[:, j, :], sb[i % NB][:, 0:256], Exp, scale=col).then_inc(sem["p%d" % j], 1)
     act.wait_ge(sem.r1, 1)
     act.activation(T.yo[:, 1, :], acc[1][:, 0:128], ActivationFunctionType.Copy, scale=T.rec[:, 1:2]).then_inc(sem.y1, 1)
     act.wait_ge(sem.y1, 1)
@@ -262,7 +244,11 @@ def rank_program(g, core, T, topo):
             pe.wait_ge(sem.lnq, 1)
         if i == 5:
             pe.wait_ge(sem.lnk, 1)
-        pe.matmul(sb[i % NB][:, 0:256], land[:, j, CK:CV], T.qs[:, :], True, True).then_inc(sem["s%d" % j], 1)
+            pe.wait_ge(sem.his, 1)
+        if i == NRAW:
+            pe.wait_ge(sem.qhs, 1)
+        pe.matmul(sb[i % NB][:, 0:256], land[:, j, CK:CV], (T.qs if i < NRAW else T.qh)[:, :], True,
+                  True).then_inc(sem["s%d" % j], 1)
 
     def weigh(i):
         j = order[i]
@@ -283,13 +269,8 @@ def rank_program(g, core, T, topo):
     pe.matmul(sb[4][:, 0:256], T.ones[:, :], T.qsq[:, :], True, True).then_inc(sem.nq, 1)
     score(1)
     score(2)
-    for g0 in range(3, NR, 3):
-        for i in range(g0, g0 + 3):
-            score(i)
-        for i in range(g0 - 3, g0):
-            weigh(i)
-    for i in range(NR - 3, NR):
-        weigh(i)
+    for kind, i in PLAN:
+        (score if kind == "S" else weigh)(i)
 
     sp.wait_ge(sem.y0, 1)
     sp.dma_start(T.y[0:128, :], T.yo[:, 0, :]).then_inc(sem.st0, 16)

from concourse.bass import DstId, RemoteDMATransfer
from concourse.mybir import AluOpType, ActivationFunctionType

NR = 12
W = 272
CL, CK, CV, C1 = 6, 8, 136, 264
NB = 6
NRAW = 5
PLAN = [("S", 3), ("S", 4), ("W", 0), ("W", 1), ("W", 2), ("S", 5), ("S", 6), ("W", 3), ("W", 4), ("S", 7), ("S", 8),
        ("W", 5), ("W", 6), ("S", 9), ("W", 7), ("W", 8), ("W", 9), ("S", 10), ("S", 11), ("W", 10), ("W", 11)]
WAVES = [[0], [1, 2], [3, 4], [5, 6, 7], [8, 9], [10, 11]]

SCRATCH = {
    "land": ("sbuf", [128, NR, W], "bfloat16"),
    "qs": ("sbuf", [128, 256], "bfloat16"),
    "qh": ("sbuf", [128, 256], "bfloat16"),
    "qsq": ("sbuf", [128, 256], "bfloat16"),
    "ksq": ("sbuf", [128, 128], "bfloat16"),
    "ones": ("sbuf", [128, 128], "bfloat16"),
    "lnb": ("sbuf", [128, 260], "float32"),
    "sc": ("sbuf", [128, 260], "float32"),
    "sk": ("sbuf", [128, NR], "float32"),
    "pp": ("sbuf", [128, NR, 256], "bfloat16"),
    "rec": ("sbuf", [128, 4], "float32"),
    "yo": ("sbuf", [128, 2, 128], "bfloat16"),
    "acc0": ("psum", [128, 512], "float32"),
    "acc1": ("psum", [128, 512], "float32"),
}
for _b in range(NB):
    SCRATCH["sb%d" % _b] = ("psum", [128, 512], "float32")

SEMAPHORES = ["ldk", "ldv", "ldq", "ms", "sqk", "sqq", "nk", "nq", "lnk", "lnq", "sce", "his", "los", "sent",
              "pv0", "pv1", "r0", "r1", "y0", "y1", "st0", "st1", "qhs"]
for _j in range(NR):
    SEMAPHORES += ["akv%d" % _j, "al%d" % _j, "s%d" % _j, "z%d" % _j, "p%d" % _j, "ske%d" % _j]


def _bits(m):
    return [e for e in range(m.bit_length()) if (m >> e) & 1]


def _mask(es):
    return sum(1 << e for e in es)


def _routes(T, topo):
    cores = list(T.cores)
    place = lambda c: (topo.host(c), topo.chip(c))
    chips = {}
    for r, c in enumerate(cores):
        chips.setdefault(place(c), []).append(r)
    routes, views = [], []
    for j, s in enumerate(cores):
        home = chips[place(s)]
        a = home.index(j)
        sw = cab = far = None
        for pl, rs in chips.items():
            d = cores[rs[0]]
            if pl == place(s):
                continue
            if topo.same_plane(s, d):
                sw = rs
            elif topo.may_write(s, d):
                cab = rs
            else:
                far = rs
        kids = {s: [cores[cab[a]], cores[sw[a]]] + [cores[r] for r in home if r != j]}
        kids[cores[sw[a]]] = [cores[r] for r in sw if r != sw[a]]
        kids[cores[cab[a]]] = [cores[far[a]]] + [cores[r] for r in cab if r != cab[a]]
        kids[cores[far[a]]] = [cores[r] for r in far if r != far[a]]
        routes.append(kids)
        views.append((home, sw, cab, far, a))
    return routes, views


def _pair(home, cores, topo):
    dies = {}
    for r in home:
        dies.setdefault(topo.die(cores[r]), []).append(r)
    many = [rs for rs in dies.values() if len(rs) > 1]
    lone = [rs for rs in dies.values() if len(rs) == 1]
    return (many[0][-1], lone[0][0]) if many and lone else (None, None)


def _split(core, dests, topo, cores):
    place = lambda c: (topo.host(c), topo.chip(c))
    low = []
    for d in cores:
        if place(d) != place(core) and topo.may_write(core, d):
            low = _bits(topo.mask(core, d))
    by = {}
    for d in dests:
        by.setdefault(place(d), []).append(d)
    away = [pl for pl in by if pl != place(core)]
    out = []
    for i, pl in enumerate(away):
        n = len(low) // len(away)
        out.append((low[i * n:(i + 1) * n], by[pl]))
    if place(core) in by:
        ds = by[place(core)]
        out.append(([e for e in _bits(topo.mask(core, ds[0])) if e not in low], ds))
    return out


def rank_program(g, core, T, topo):
    cores = list(T.cores)
    me = T.rank_of(core)
    if me is None:
        return
    routes, views = _routes(T, topo)
    sem = T.sem
    land = T.land
    place = lambda c: (topo.host(c), topo.chip(c))
    home, sw, cab, far, a = views[me]
    donor, relay = _pair(home, cores, topo)

    nkv, nl = {}, {}
    for j, kids in enumerate(routes):
        for snd, ds in kids.items():
            for es, grp in _split(snd, ds, topo, cores):
                if core in grp:
                    nkv[j] = len(es)
                    nl[j] = len(es) if snd == cores[j] else 0
    if cab[a] == _pair(cab, cores, topo)[0]:
        nkv[cab[a]] *= 2

    sent = [0]

    def call(parts, j, c0, c1, rsem):
        trs = []
        for es, grp in parts:
            ids = []
            for d in grp:
                rid, pid = topo.addr(d, core)
                ids.append(DstId(rid=rid, pnc=pid))
            trs.append(RemoteDMATransfer(dst_ids=ids, dma_engine_mask=_mask(es), remote_sem=rsem,
                                         srcs=[land[:, j, c0:c1]], dsts=[land[:, j, c0:c1] for _ in grp], alu_op=0))
            sent[0] += len(es)
        g.remote_dma_fused(trs, local_sem=sem.sent)

    def forwards():
        js = [j for j, kids in enumerate(routes) if core in kids and cores[j] != core]
        js.sort(key=lambda j: 0 if any(place(d) != place(core) for d in routes[j][core]) else (1 if nl[j] else 2))
        for j in js:
            g.wait_ge(sem["akv%d" % j], nkv[j])
            if nl[j]:
                g.wait_ge(sem["al%d" % j], nl[j])
            call(_split(core, routes[j][core], topo, cores), j, CL, C1, sem["akv%d" % j])
        g.wait_ge(sem.sent, sent[0])

    Exp, Ln = ActivationFunctionType.Exp, ActivationFunctionType.Ln
    pe, dve, act, sp = g.tensor, g.vector, g.scalar, g.sync
    sb = [T["sb%d" % b] for b in range(NB)]
    acc = [T.acc0, T.acc1]

    order = [me] + [r for r in home if r != me] + [sw[a], cab[a]] + [r for r in cab if r != cab[a]] \
        + [far[a]] + [r for r in sw if r != sw[a]] + [r for r in far if r != far[a]]

    sp.dma_start(land[:, me, CK:CV], T.k[:, :]).then_inc(sem.ldk, 16)
    act.dma_start(land[:, me, CV:C1], T.v[:, :]).then_inc(sem.ldv, 16)
    sp.dma_start(T.qs[:, :], T.q[:, :]).then_inc(sem.ldq, 16)

    mine = _split(core, routes[me][core], topo, cores)
    off = [p for p in mine if place(p[1][0]) != place(core)]
    on = [p for p in mine if place(p[1][0]) == place(core)]
    g.wait_ge(sem.ldk, 16)
    g.wait_ge(sem.ldv, 16)
    if me == donor:
        call(off[1:] + on, me, CK, C1, sem["akv%d" % me])
        call(off[:1], me, CK, CV, sem["akv%d" % me])
    else:
        call(off, me, CK, C1, sem["akv%d" % me])
        call(on, me, CK, C1, sem["akv%d" % me])
    if me == relay:
        g.wait_ge(sem["akv%d" % donor], nkv[donor])
        call([(off[0][0], [cores[views[donor][2][views[donor][4]]]])], donor, CV, C1, sem["akv%d" % donor])
    g.wait_ge(sem.his, 1)
    g.wait_ge(sem.los, 1)
    call(mine, me, CL, CK, sem["al%d" % me])
    forwards()

    dve.memset(T.ones[:, :], 1.0).then_inc(sem.ms, 1)
    dve.memset(land[:, :, C1:W], 1.0).then_inc(sem.ms, 1)
    dve.wait_ge(sem.ldq, 16)
    dve.tensor_tensor(T.qsq[:, :], T.qs[:, :], T.qs[:, :], AluOpType.mult).then_inc(sem.sqq, 1)
    dve.wait_ge(sem.lnk, 1)
    dve.wait_ge(sem.his, 1)
    dve.tensor_scalar(land[:, me, CL + 1:CK], T.lnb[:, 256:257], land[:, me, CL:CL + 1], -0.5,
                      AluOpType.subtract, AluOpType.mult).then_inc(sem.los, 1)
    for i in range(NRAW):
        j, t = order[i], sb[i % NB]
        dve.wait_ge(sem["s%d" % j], 1)
        if i == 0:
            dve.wait_ge(sem.sce, 1)
        dve.tensor_tensor(t[:, 0:256], t[:, 0:256], T.sc[:, 0:256], AluOpType.mult).then_inc(sem["z%d" % j], 1)
        if i == 2:
            dve.tensor_tensor(T.qh[:, :], T.qs[:, :], T.sc[:, 0:256], AluOpType.mult).then_inc(sem.qhs, 1)
    dve.wait_ge(sem.pv0, 1)
    dve.reciprocal(T.rec[:, 0:1], acc[0][:, 128:129]).then_inc(sem.r0, 1)
    dve.wait_ge(sem.pv1, 1)
    dve.reciprocal(T.rec[:, 1:2], acc[1][:, 128:129]).then_inc(sem.r1, 1)
    dve.wait_ge(sem.r0, 1)
    dve.tensor_scalar(T.yo[:, 0, :], acc[0][:, 0:128], T.rec[:, 0:1], None, AluOpType.mult).then_inc(sem.y0, 1)

    act.wait_ge(sem.ldk, 16)
    act.activation(T.ksq[:, :], land[:, me, CK:CV], ActivationFunctionType.Square).then_inc(sem.sqk, 1)
    act.wait_ge(sem.nk, 1)
    act.activation(T.lnb[:, 256:257], sb[5][:, 0:1], Ln, scale=1.0 / 16).then_inc(sem.lnk, 1)
    act.activation(land[:, me, CL:CL + 1], sb[5][:, 0:1], Ln, scale=1.0 / 16).then_inc(sem.his, 1)
    act.wait_ge(sem.nq, 1)
    act.activation(T.lnb[:, 0:256], sb[4][:, 0:256], Ln, scale=1.0 / 16).then_inc(sem.lnq, 1)
    act.wait_ge(sem.lnk, 1)
    act.wait_ge(sem.lnq, 1)
    act.activation(T.sc[:, 0:257], T.lnb[:, 0:257], Exp, scale=-0.5).then_inc(sem.sce, 1)
    act.wait_ge(sem.sce, 1)
    for wave in WAVES:
        for i in wave:
            j = order[i]
            if j != me:
                act.wait_ge(sem[("al%d" if nl[j] else "akv%d") % j], nl[j] or nkv[j])
                act.activation(T.sk[:, j:j + 1], land[:, j, CL:CL + 1], Exp, bias=land[:, j, CL + 1:CK],
                               scale=-0.5).then_inc(sem["ske%d" % j], 1)
        for i in wave:
            j = order[i]
            if j != me:
                act.wait_ge(sem["ske%d" % j], 1)
            col = T.sk[:, j:j + 1] if j != me else T.sc[:, 256:257]
            act.wait_ge(sem[("z%d" if i < NRAW else "s%d") % j], 1)
            act.activation(T.pp[:, j, :], sb[i % NB][:, 0:256], Exp, scale=col).then_inc(sem["p%d" % j], 1)
    act.wait_ge(sem.r1, 1)
    act.activation(T.yo[:, 1, :], acc[1][:, 0:128], ActivationFunctionType.Copy, scale=T.rec[:, 1:2]).then_inc(sem.y1, 1)
    act.wait_ge(sem.y1, 1)
    act.dma_start(T.y[128:256, :], T.yo[:, 1, :]).then_inc(sem.st1, 16)
    act.wait_ge(sem.st1, 16)

    def score(i):
        j = order[i]
        if j == me:
            pe.wait_ge(sem.ldk, 16)
            pe.wait_ge(sem.ldq, 16)
        else:
            pe.wait_ge(sem["akv%d" % j], nkv[j])
        if i == 4:
            pe.wait_ge(sem.lnq, 1)
        if i == 5:
            pe.wait_ge(sem.lnk, 1)
            pe.wait_ge(sem.his, 1)
        if i == NRAW:
            pe.wait_ge(sem.qhs, 1)
        pe.matmul(sb[i % NB][:, 0:256], land[:, j, CK:CV], (T.qs if i < NRAW else T.qh)[:, :], True,
                  True).then_inc(sem["s%d" % j], 1)

    def weigh(i):
        j = order[i]
        pe.wait_ge(sem["p%d" % j], 1)
        if j == me:
            pe.wait_ge(sem.ldv, 16)
        for h in range(2):
            m = pe.matmul(acc[h][:, 0:129], T.pp[:, j, 128 * h:128 * h + 128], land[:, j, CV:C1 + 1],
                          i == 0, i == NR - 1)
            if i == NR - 1:
                m.then_inc(sem["pv%d" % h], 1)

    pe.wait_ge(sem.ms, 2)
    pe.wait_ge(sem.sqk, 1)
    pe.matmul(sb[5][:, 0:1], T.ksq[:, :], T.ones[:, 0:1], True, True).then_inc(sem.nk, 1)
    score(0)
    pe.wait_ge(sem.sqq, 1)
    pe.matmul(sb[4][:, 0:256], T.ones[:, :], T.qsq[:, :], True, True).then_inc(sem.nq, 1)
    score(1)
    score(2)
    for kind, i in PLAN:
        (score if kind == "S" else weigh)(i)

    sp.wait_ge(sem.y0, 1)
    sp.dma_start(T.y[0:128, :], T.yo[:, 0, :]).then_inc(sem.st0, 16)
    sp.wait_ge(sem.st0, 16)
